import numpy as np
import ml_dtypes


def mxq(x, axis, fmt="e4m3"):
    dtype, down = {"e4m3": (ml_dtypes.float8_e4m3fn, 7), "e5m2": (ml_dtypes.float8_e5m2, 14)}[fmt]
    v = np.moveaxis(np.asarray(x, np.float32).astype(ml_dtypes.bfloat16).astype(np.float64), axis, -1)
    blocks = v.reshape(v.shape[:-1] + (-1, 32))
    amax = np.abs(blocks).max(-1, keepdims=True)
    byte = np.maximum(np.where(amax > 0, np.frexp(amax)[1] - 1 + 127, 0) - down, 1)
    scale = np.exp2(byte - 127.0)
    codes = (blocks / scale).astype(np.float32).astype(dtype).astype(np.float64)
    return np.moveaxis((codes * scale).reshape(v.shape), -1, axis)


WIDE = False


def mx_kscale(k):
    if not WIDE:
        return np.ones(k)
    levels = np.array([10, -10, 5, -5, 0])
    if k % 512:
        return np.exp2(np.random.permutation(np.resize(levels, k // 32))).repeat(32)
    a = np.empty((k // 512, 16))
    for p in range(k // 512):
        a[p, :8] = np.random.permutation(np.resize(levels, 8))
        for g in range(8):
            far = levels[np.abs(levels - a[p, g]) >= 10]
            a[p, g + 8] = far[np.random.randint(len(far))]
    return np.exp2(a.ravel()).repeat(32)


def f64(x):
    return np.asarray(x).astype(np.float64)


def striped(idx):
    return np.tile(np.asarray(idx).reshape(-1, 16).T, (8, 1)).astype(np.uint16)


def unstriped(offs):
    return offs[:16].T.reshape(-1).astype(np.int64)


def striped8(idx):
    return np.asarray(idx).reshape(8, -1, 16).transpose(0, 2, 1).reshape(128, -1).astype(np.uint16)


def unstriped8(offs):
    return offs.reshape(8, 16, -1).transpose(0, 2, 1).reshape(8, -1).astype(np.int64)


def pick8(x, idx, run):
    r = np.arange(len(x))
    return x[r[:, None], idx[r % (8 * run) // run]]


E2M1 = np.array([0.0, 0.5, 1.0, 1.5, 2.0, 3.0, 4.0, 6.0, -0.0, -0.5, -1.0, -1.5, -2.0, -3.0, -4.0, -6.0])


def pack_weight(w, fmt):
    k, n = w.shape
    w = f64(np.asarray(w, np.float32).astype(ml_dtypes.bfloat16)).reshape(k // 32, 32, n)
    amax = np.abs(w).max(1)
    if fmt == "e4m3":
        byte = np.frexp(amax)[1] - 1 + 127 - 7
    else:
        mant, ex = np.frexp(amax / 6.0)
        byte = np.where(mant > 0.5, ex, ex - 1) + 127
    byte = np.clip(np.where(amax > 0, byte, 1), 1, 254)
    scaled = (w * np.exp2(127.0 - byte)[:, None, :]).reshape(k, n).astype(np.float32)
    by_word = np.ascontiguousarray(scaled.reshape(k // 512, 128, 4, n).transpose(0, 1, 3, 2))
    if fmt == "e4m3":
        words = by_word.astype(ml_dtypes.float8_e4m3fn).view(np.uint8)
    else:
        c = by_word.astype(ml_dtypes.float4_e2m1fn).view(np.uint8) & 0xF
        words = (c[..., 0::2] | (c[..., 1::2] << 4)).reshape(k // 512, 128, 2 * n)
    return np.ascontiguousarray(words), np.ascontiguousarray(byte.astype(np.uint8).reshape(k // 512, 16, n))


def unpack_weight(words, scales, fmt):
    g, _, n = scales.shape
    words = np.ascontiguousarray(words).reshape(g, 128, n, -1)
    if fmt == "e4m3":
        vals = words.view(ml_dtypes.float8_e4m3fn).astype(np.float64)
    else:
        nib = np.empty((g, 128, n, 4), np.uint8)
        nib[..., 0::2] = words & 0xF
        nib[..., 1::2] = words >> 4
        vals = E2M1[nib]
    vals = vals * np.repeat(np.exp2(scales.astype(np.float64) - 127.0), 8, axis=1)[..., None]
    return vals.transpose(0, 1, 3, 2).reshape(g * 512, n)


K, J, R, T, F, C, O, S, N = 512, 256, 512, 1024, 1024, 512, 128, 256, 256


def setup_inputs():
    n = np.random.standard_normal
    idx = np.stack([np.random.permutation(T)[:J] for _ in range(8)])
    idx2 = np.stack([np.random.permutation(T)[:J] for _ in range(8)])
    idx3 = np.random.permutation(F)[:R]
    idx4 = np.stack([np.random.permutation(C)[:J] for _ in range(8)])
    idx5 = np.stack([np.random.permutation(C)[:S] for _ in range(8)])
    idx6 = np.random.permutation(C)[:S]
    idx7 = np.stack([np.random.permutation(S)[:O] for _ in range(8)])
    fk = mx_kscale(K)
    fr = mx_kscale(R)
    tr = np.ones(F)
    tr[idx3] = fr
    wtp = pack_weight(n((K, F)) * 1 / np.sqrt(K) / fk[:, None] * tr, "e4m3")
    wbp = pack_weight(n((R, N)) * 1 / np.sqrt(R) / fr[:, None], "e2m1")
    return {
        "ta": (np.random.randint(-7, 8, (K, T)).astype(np.float64)).astype(np.float32),
        "ga": ((np.random.randint(8, 19, (K, 1)) / 64.0) * fk[:, None]).astype(np.float32),
        "gb": ((np.random.randint(8, 19, (K, 1)) / 64.0) * fk[:, None]).astype(np.float32),
        "wt_words": wtp[0],
        "wt_scales": wtp[1],
        "sa": (np.random.uniform(0.5, 1.6, (R, 1))).astype(np.float32),
        "sb": (np.random.uniform(0.5, 1.6, (R, 1))).astype(np.float32),
        "sd": (np.random.uniform(0.5, 1.6, (R, 1))).astype(np.float32),
        "wb_words": wbp[0],
        "wb_scales": wbp[1],
        "offs": striped8(idx),
        "offs2": striped8(idx2),
        "offs3": striped(idx3),
        "offs4": striped8(idx4),
        "offs5": striped8(idx5),
        "offs6": striped(idx6),
        "offs7": striped8(idx7),
    }


def reference(ta, ga, gb, wt_words, wt_scales, sa, sb, sd, wb_words, wb_scales, offs, offs2, offs3, offs4, offs5, offs6, offs7):
    idx = unstriped8(offs)
    idx2 = unstriped8(offs2)
    idx3 = unstriped(offs3)
    idx4 = unstriped8(offs4)
    idx5 = unstriped8(offs5)
    idx6 = unstriped(offs6)
    idx7 = unstriped8(offs7)
    wtu = unpack_weight(wt_words, wt_scales, "e4m3")
    wbu = unpack_weight(wb_words, wb_scales, "e2m1")
    xc = pick8(f64(ta), idx, 64) * f64(ga) - pick8(f64(ta), idx2, 64) * f64(gb)
    wtidx3g = wtu[:, idx3]
    xcq = mxq(xc, 0, "e4m3")
    a = wtidx3g.T @ xcq
    pw = np.zeros((R, C))
    pw[np.arange(R)[:, None], idx4[np.arange(R) % 512 // 64]] = a
    pg = np.maximum(pick8(pw, idx5, 64) * f64(sa), pw[:, idx6] * f64(sb))
    hid = pick8(pg, idx7, 64) * f64(sd)
    hidq = mxq(hid, 0, "e4m3")
    y = wbu.T @ hidq
    return y

@@ -1,0 +1,162 @@
+from contextlib import ExitStack
+
+import concourse.mybir as mybir
+
+K, J, R, T, F, C, O, S, N = 512, 256, 512, 1024, 1024, 512, 128, 256, 256
+P = 128
+PACK = 4
+HALF = J // 2
+
+F32 = mybir.dt.float32
+BF16 = mybir.dt.bfloat16
+I32 = mybir.dt.int32
+U32 = mybir.dt.uint32
+U16 = mybir.dt.uint16
+U8 = mybir.dt.uint8
+FP8X4 = mybir.dt.float8_e4m3fn_x4
+FP4X4 = mybir.dt.float4_e2m1fn_x4
+COPY = mybir.ActivationFunctionType.Copy
+SUB = mybir.AluOpType.subtract
+MAX = mybir.AluOpType.max
+
+FLOPS = 2 * K * R * J + 2 * R * N * O
+
+
+def tile_picked_codegap_store_one_ladder_one_plain_kernel(
+    tc, ta, ga, gb, wt_words, wt_scales, sa, sb, sd, wb_words, wb_scales,
+    offs, offs2, offs3, offs4, offs5, offs6, offs7, out,
+):
+    nc = tc.nc
+    with ExitStack() as ctx:
+        keep = ctx.enter_context(tc.tile_pool(name="keep", bufs=1))
+        psum = ctx.enter_context(tc.psum_pool(name="psum", bufs=1))
+
+        def load_list(name, src):
+            tile = keep.tile(list(src.shape), U16, name=name)
+            nc.sync.dma_start(tile[:], src)
+            return tile
+
+        def load_column(name, src):
+            tile = keep.tile([P, PACK], F32, name=name)
+            nc.sync.dma_start(tile[:], src.rearrange("(p t) one -> p (t one)", t=PACK))
+            return tile
+
+        ta_rows = ta.rearrange("(p t) c -> p t c", t=PACK)
+        ta_sb = [keep.tile([P, T], F32, name="ta%d" % t) for t in range(PACK)]
+
+        wts_stage = keep.tile([P, 2, F], U8, name="wts_stage")
+        for half in range(2):
+            nc.scalar.dma_start(
+                wts_stage[64 * half : 64 * half + 4, :, :].bitcast(I32),
+                wt_scales[0, 8 * half : 8 * half + 8, :].bitcast(I32).rearrange("(q i) c -> i q c", i=4),
+            )
+        nc.sync.dma_start(ta_sb[0][:], ta_rows[:, 0, :])
+        l1 = load_list("l1", offs)
+        ga_sb = load_column("ga_sb", ga)
+        l2 = load_list("l2", offs2)
+        gb_sb = load_column("gb_sb", gb)
+        nc.sync.dma_start(ta_sb[1][:], ta_rows[:, 1, :])
+        l3 = load_list("l3", offs3)
+        wtw = keep.tile([P, F], U32, name="wtw")
+        nc.sync.dma_start(wtw[:].bitcast(I32), wt_words[0].rearrange("p c t -> p (c t)").bitcast(I32))
+        for t in range(2, PACK):
+            nc.sync.dma_start(ta_sb[t][:], ta_rows[:, t, :])
+        l4 = load_list("l4", offs4)
+        l5 = load_list("l5", offs5)
+        sa_sb = load_column("sa_sb", sa)
+        l6 = load_list("l6", offs6)
+        sb_sb = load_column("sb_sb", sb)
+        l7 = load_list("l7", offs7)
+        sd_sb = load_column("sd_sb", sd)
+        wbw = keep.tile([P, 2 * N], U8, name="wbw", align_bytes=64)
+        nc.sync.dma_start(wbw[:].bitcast(I32), wb_words[0].bitcast(I32))
+
+        wts = keep.tile([P, F], U8, name="wts")
+        nc.vector.memset(wts[:].bitcast(I32), 0)
+        wbs = keep.tile([P, N], U8, name="wbs", align_bytes=64)
+        nc.vector.memset(wbs[:].bitcast(I32), 0)
+        for q in range(4):
+            nc.sync.dma_start(wbs[32 * q : 32 * q + 4, :].bitcast(I32), wb_scales[0, 4 * q : 4 * q + 4, :].bitcast(I32))
+        pw = [keep.tile([P, C], F32, name="pw%d" % t) for t in range(PACK)]
+        for t in range(PACK):
+            nc.vector.memset(pw[t][:], 0.0)
+
+        for q in range(4):
+            src = 64 * (q // 2)
+            nc.vector.tensor_copy(wts[32 * q : 32 * q + 4, :].bitcast(I32), wts_stage[src : src + 4, q % 2, :].bitcast(I32))
+        picked_s = keep.tile([P, R], U8, name="picked_s")
+        nc.vector.tensor_copy(picked_s[:], wts[:].indirect(l3[:]))
+        dealt_s = keep.tile([P, PACK, P], U8, name="dealt_s", align_bytes=64)
+        picked_w = keep.tile([P, R], U32, name="picked_w")
+        nc.vector.tensor_copy(picked_w[:], wtw[:].indirect(l3[:]))
+        nc.vector.tensor_copy(dealt_s[:], picked_s[:].rearrange("p (m t) -> p t m", t=PACK))
+        dealt_w = keep.tile([P, PACK, P], U32, name="dealt_w", align_bytes=64)
+        nc.vector.tensor_copy(dealt_w[:].bitcast(I32), picked_w[:].bitcast(I32).rearrange("p (m t) -> p t m", t=PACK))
+
+        xc = [keep.tile([P, HALF, PACK], BF16, name="xc%d" % h, align_bytes=64) for h in range(2)]
+        xq = keep.tile([P, J], U32, name="xq", align_bytes=64)
+        xs = keep.tile([P, J], U8, name="xs", align_bytes=64)
+        halves = [slice(0, HALF), slice(HALF, J)]
+        for pair in range(2):
+            first = keep.tile([P, 2, J], F32, name="first%d" % pair)
+            second = keep.tile([P, 2, J], F32, name="second%d" % pair)
+            for e in range(2):
+                t = 2 * pair + e
+                nc.scalar.activation(first[:, e, :], ta_sb[t][:].indirect(l1[:]), COPY, scale=ga_sb[:, t : t + 1])
+                nc.scalar.activation(second[:, e, :], ta_sb[t][:].indirect(l2[:]), COPY, scale=gb_sb[:, t : t + 1])
+            for h, cols in enumerate(halves):
+                nc.vector.tensor_tensor(
+                    xc[h][:, :, 2 * pair : 2 * pair + 2].rearrange("p (c i) e -> p c e i", i=4),
+                    first[:, :, cols].rearrange("p e (c i) -> p c e i", i=4),
+                    second[:, :, cols].rearrange("p e (c i) -> p c e i", i=4),
+                    SUB,
+                )
+                if pair == 1:
+                    nc.vector.quantize_mx(
+                        out=xq[:, cols].bitcast(FP8X4), scales=xs[:, cols], in_=xc[h][:].rearrange("p j t -> p (j t)")
+                    )
+
+        pieces = [(0, 0, HALF), (1, 0, J), (0, HALF, J)] + [(t, 0, J) for t in range(2, PACK)]
+        a_sb = []
+        for i, (t, lo, hi) in enumerate(pieces):
+            acc = psum.tile([P, hi - lo], F32, name="acc%d" % i)
+            nc.tensor.matmul_mx(
+                out=acc[:], lhsT=dealt_w[:, t, :].bitcast(FP8X4), lhsT_scale=dealt_s[:, t, :],
+                rhs=xq[:, lo:hi].bitcast(FP8X4), rhs_scale=xs[:, lo:hi], start=True, stop=True,
+            )
+            piece = keep.tile([P, hi - lo], F32, name="a%d" % i)
+            nc.scalar.copy(piece[:], acc[:])
+            a_sb.append(piece)
+        for (t, lo, hi), piece in zip(pieces, a_sb):
+            nc.vector.tensor_copy(pw[t][:].indirect(l4[:, lo // 16 : hi // 16]), piece[:])
+
+        own = [keep.tile([P, S], F32, name="own%d" % t) for t in range(PACK)]
+        shared = [keep.tile([P, S], F32, name="shared%d" % t) for t in range(PACK)]
+        for t in (1, 0, 2, 3):
+            nc.scalar.activation(own[t][:], pw[t][:].indirect(l5[:]), COPY, scale=sa_sb[:, t : t + 1])
+            nc.scalar.activation(shared[t][:], pw[t][:].indirect(l6[:]), COPY, scale=sb_sb[:, t : t + 1])
+        hid = keep.tile([P, PACK, O], BF16, name="hid")
+        hx = keep.tile([P, O, PACK], BF16, name="hx", align_bytes=64)
+        for t in range(PACK):
+            pg = keep.tile([P, S], F32, name="pg%d" % t)
+            nc.vector.tensor_tensor(pg[:], own[t][:], shared[t][:], MAX)
+            nc.scalar.activation(hid[:, t, :], pg[:].indirect(l7[:]), COPY, scale=sd_sb[:, t : t + 1])
+        for t in range(0, PACK, 2):
+            nc.vector.tensor_copy(hx[:, :, t : t + 2], hid[:, t : t + 2, :].rearrange("p t o -> p o t"))
+        hq = keep.tile([P, O], U32, name="hq", align_bytes=64)
+        hs = keep.tile([P, O], U8, name="hs", align_bytes=64)
+        nc.vector.quantize_mx(out=hq[:].bitcast(FP8X4), scales=hs[:], in_=hx[:].rearrange("p o t -> p (o t)"))
+
+        for u in range(N // P):
+            acc = psum.tile([P, O], F32, name="y%d" % u)
+            nc.tensor.matmul_mx(
+                out=acc[:], lhsT=wbw[:, 2 * P * u : 2 * P * (u + 1)].bitcast(FP4X4), lhsT_scale=wbs[:, P * u : P * (u + 1)],
+                rhs=hq[:].bitcast(FP8X4), rhs_scale=hs[:], start=True, stop=True,
+            )
+            res = keep.tile([P, O], F32, name="res%d" % u)
+            if u == 0:
+                nc.vector.tensor_copy(res[:], acc[:])
+                nc.sync.dma_start(out[P * u : P * (u + 1), :], res[:])
+            else:
+                nc.scalar.copy(res[:], acc[:])
+                nc.scalar.dma_start(out[P * u : P * (u + 1), :], res[:])

@@ -50,6 +50,9 @@ def tile_picked_codegap_store_one_ladder_one_plain_kernel(
                 wts_stage[64 * half : 64 * half + 4, :, :].bitcast(I32),
                 wt_scales[0, 8 * half : 8 * half + 8, :].bitcast(I32).rearrange("(q i) c -> i q c", i=4),
             )
+        warm = keep.tile([P, 2], F32, name="warm")
+        nc.gpsimd.memset(warm[:, 0:1], 0.0)
+        nc.scalar.activation(warm[:, 1:2], warm[:, 0:1], COPY)
         nc.sync.dma_start(ta_sb[0][:], ta_rows[:, 0, :])
         l1 = load_list("l1", offs)
         ga_sb = load_column("ga_sb", ga)

@@ -36,9 +36,9 @@ def tile_picked_codegap_store_one_ladder_one_plain_kernel(
             nc.sync.dma_start(tile[:], src)
             return tile
 
-        def load_column(name, src):
+        def load_column(name, src, queue):
             tile = keep.tile([P, PACK], F32, name=name)
-            nc.sync.dma_start(tile[:], src.rearrange("(p t) one -> p (t one)", t=PACK))
+            queue.dma_start(tile[:], src.rearrange("(p t) one -> p (t one)", t=PACK))
             return tile
 
         ta_rows = ta.rearrange("(p t) c -> p t c", t=PACK)
@@ -53,24 +53,24 @@ def tile_picked_codegap_store_one_ladder_one_plain_kernel(
         warm = keep.tile([P, 2], F32, name="warm")
         nc.gpsimd.memset(warm[:, 0:1], 0.0)
         nc.scalar.activation(warm[:, 1:2], warm[:, 0:1], COPY)
+        l3 = load_list("l3", offs3)
         nc.sync.dma_start(ta_sb[0][:], ta_rows[:, 0, :])
         l1 = load_list("l1", offs)
-        ga_sb = load_column("ga_sb", ga)
+        ga_sb = load_column("ga_sb", ga, nc.scalar)
         l2 = load_list("l2", offs2)
-        gb_sb = load_column("gb_sb", gb)
         nc.sync.dma_start(ta_sb[1][:], ta_rows[:, 1, :])
-        l3 = load_list("l3", offs3)
+        gb_sb = load_column("gb_sb", gb, nc.sync)
         wtw = keep.tile([P, F], U32, name="wtw")
         nc.sync.dma_start(wtw[:].bitcast(I32), wt_words[0].rearrange("p c t -> p (c t)").bitcast(I32))
         for t in range(2, PACK):
             nc.sync.dma_start(ta_sb[t][:], ta_rows[:, t, :])
         l4 = load_list("l4", offs4)
         l5 = load_list("l5", offs5)
-        sa_sb = load_column("sa_sb", sa)
+        sa_sb = load_column("sa_sb", sa, nc.sync)
         l6 = load_list("l6", offs6)
-        sb_sb = load_column("sb_sb", sb)
+        sb_sb = load_column("sb_sb", sb, nc.sync)
         l7 = load_list("l7", offs7)
-        sd_sb = load_column("sd_sb", sd)
+        sd_sb = load_column("sd_sb", sd, nc.sync)
         wbw = keep.tile([P, 2 * N], U8, name="wbw", align_bytes=64)
         nc.sync.dma_start(wbw[:].bitcast(I32), wb_words[0].bitcast(I32))
 

from contextlib import ExitStack

import concourse.mybir as mybir

K, J, R, T, F, C, O, S, N = 512, 256, 512, 1024, 1024, 512, 128, 256, 256
P = 128
PACK = 4
HALF = J // 2

F32 = mybir.dt.float32
BF16 = mybir.dt.bfloat16
I32 = mybir.dt.int32
U32 = mybir.dt.uint32
U16 = mybir.dt.uint16
U8 = mybir.dt.uint8
FP8X4 = mybir.dt.float8_e4m3fn_x4
FP4X4 = mybir.dt.float4_e2m1fn_x4
COPY = mybir.ActivationFunctionType.Copy
SUB = mybir.AluOpType.subtract
MAX = mybir.AluOpType.max

FLOPS = 2 * K * R * J + 2 * R * N * O


def tile_picked_codegap_store_one_ladder_one_plain_kernel(
    tc, ta, ga, gb, wt_words, wt_scales, sa, sb, sd, wb_words, wb_scales,
    offs, offs2, offs3, offs4, offs5, offs6, offs7, out,
):
    nc = tc.nc
    with ExitStack() as ctx:
        keep = ctx.enter_context(tc.tile_pool(name="keep", bufs=1))
        psum = ctx.enter_context(tc.psum_pool(name="psum", bufs=1))

        def load_list(name, src):
            tile = keep.tile(list(src.shape), U16, name=name)
            nc.sync.dma_start(tile[:], src)
            return tile

        def load_column(name, src, queue):
            tile = keep.tile([P, PACK], F32, name=name)
            queue.dma_start(tile[:], src.rearrange("(p t) one -> p (t one)", t=PACK))
            return tile

        ta_rows = ta.rearrange("(p t) c -> p t c", t=PACK)
        ta_sb = [keep.tile([P, T], F32, name="ta%d" % t) for t in range(PACK)]

        wts_stage = keep.tile([P, 2, F], U8, name="wts_stage")
        for half in range(2):
            nc.scalar.dma_start(
                wts_stage[64 * half : 64 * half + 4, :, :].bitcast(I32),
                wt_scales[0, 8 * half : 8 * half + 8, :].bitcast(I32).rearrange("(q i) c -> i q c", i=4),
            )
        warm = keep.tile([P, 2], F32, name="warm")
        nc.gpsimd.memset(warm[:, 0:1], 0.0)
        nc.scalar.activation(warm[:, 1:2], warm[:, 0:1], COPY)
        l3 = load_list("l3", offs3)
        nc.sync.dma_start(ta_sb[0][:], ta_rows[:, 0, :])
        l1 = load_list("l1", offs)
        ga_sb = load_column("ga_sb", ga, nc.scalar)
        l2 = load_list("l2", offs2)
        nc.sync.dma_start(ta_sb[1][:], ta_rows[:, 1, :])
        gb_sb = load_column("gb_sb", gb, nc.sync)
        wtw = keep.tile([P, F], U32, name="wtw")
        nc.sync.dma_start(wtw[:].bitcast(I32), wt_words[0].rearrange("p c t -> p (c t)").bitcast(I32))
        for t in range(2, PACK):
            nc.sync.dma_start(ta_sb[t][:], ta_rows[:, t, :])
        l4 = load_list("l4", offs4)
        l5 = load_list("l5", offs5)
        sa_sb = load_column("sa_sb", sa, nc.sync)
        l6 = load_list("l6", offs6)
        sb_sb = load_column("sb_sb", sb, nc.sync)
        l7 = load_list("l7", offs7)
        sd_sb = load_column("sd_sb", sd, nc.sync)
        wbw = keep.tile([P, 2 * N], U8, name="wbw", align_bytes=64)
        nc.sync.dma_start(wbw[:].bitcast(I32), wb_words[0].bitcast(I32))

        wts = keep.tile([P, F], U8, name="wts")
        nc.vector.memset(wts[:].bitcast(I32), 0)
        wbs = keep.tile([P, N], U8, name="wbs", align_bytes=64)
        nc.vector.memset(wbs[:].bitcast(I32), 0)
        for q in range(4):
            nc.sync.dma_start(wbs[32 * q : 32 * q + 4, :].bitcast(I32), wb_scales[0, 4 * q : 4 * q + 4, :].bitcast(I32))
        pw = [keep.tile([P, C], F32, name="pw%d" % t) for t in range(PACK)]
        for t in range(PACK):
            nc.vector.memset(pw[t][:], 0.0)

        for q in range(4):
            src = 64 * (q // 2)
            nc.vector.tensor_copy(wts[32 * q : 32 * q + 4, :].bitcast(I32), wts_stage[src : src + 4, q % 2, :].bitcast(I32))
        picked_s = keep.tile([P, R], U8, name="picked_s")
        nc.vector.tensor_copy(picked_s[:], wts[:].indirect(l3[:]))
        dealt_s = keep.tile([P, PACK, P], U8, name="dealt_s", align_bytes=64)
        picked_w = keep.tile([P, R], U32, name="picked_w")
        nc.vector.tensor_copy(picked_w[:], wtw[:].indirect(l3[:]))
        nc.vector.tensor_copy(dealt_s[:], picked_s[:].rearrange("p (m t) -> p t m", t=PACK))
        dealt_w = keep.tile([P, PACK, P], U32, name="dealt_w", align_bytes=64)
        nc.vector.tensor_copy(dealt_w[:].bitcast(I32), picked_w[:].bitcast(I32).rearrange("p (m t) -> p t m", t=PACK))

        xc = [keep.tile([P, HALF, PACK], BF16, name="xc%d" % h, align_bytes=64) for h in range(2)]
        xq = keep.tile([P, J], U32, name="xq", align_bytes=64)
        xs = keep.tile([P, J], U8, name="xs", align_bytes=64)
        halves = [slice(0, HALF), slice(HALF, J)]
        for pair in range(2):
            first = keep.tile([P, 2, J], F32, name="first%d" % pair)
            second = keep.tile([P, 2, J], F32, name="second%d" % pair)
            for e in range(2):
                t = 2 * pair + e
                nc.scalar.activation(first[:, e, :], ta_sb[t][:].indirect(l1[:]), COPY, scale=ga_sb[:, t : t + 1])
                nc.scalar.activation(second[:, e, :], ta_sb[t][:].indirect(l2[:]), COPY, scale=gb_sb[:, t : t + 1])
            for h, cols in enumerate(halves):
                nc.vector.tensor_tensor(
                    xc[h][:, :, 2 * pair : 2 * pair + 2].rearrange("p (c i) e -> p c e i", i=4),
                    first[:, :, cols].rearrange("p e (c i) -> p c e i", i=4),
                    second[:, :, cols].rearrange("p e (c i) -> p c e i", i=4),
                    SUB,
                )
                if pair == 1:
                    nc.vector.quantize_mx(
                        out=xq[:, cols].bitcast(FP8X4), scales=xs[:, cols], in_=xc[h][:].rearrange("p j t -> p (j t)")
                    )

        pieces = [(0, 0, HALF), (1, 0, J), (0, HALF, J)] + [(t, 0, J) for t in range(2, PACK)]
        a_sb = []
        for i, (t, lo, hi) in enumerate(pieces):
            acc = psum.tile([P, hi - lo], F32, name="acc%d" % i)
            nc.tensor.matmul_mx(
                out=acc[:], lhsT=dealt_w[:, t, :].bitcast(FP8X4), lhsT_scale=dealt_s[:, t, :],
                rhs=xq[:, lo:hi].bitcast(FP8X4), rhs_scale=xs[:, lo:hi], start=True, stop=True,
            )
            piece = keep.tile([P, hi - lo], F32, name="a%d" % i)
            nc.scalar.copy(piece[:], acc[:])
            a_sb.append(piece)
        for (t, lo, hi), piece in zip(pieces, a_sb):
            nc.vector.tensor_copy(pw[t][:].indirect(l4[:, lo // 16 : hi // 16]), piece[:])

        own = [keep.tile([P, S], F32, name="own%d" % t) for t in range(PACK)]
        shared = [keep.tile([P, S], F32, name="shared%d" % t) for t in range(PACK)]
        for t in (1, 0, 2, 3):
            nc.scalar.activation(own[t][:], pw[t][:].indirect(l5[:]), COPY, scale=sa_sb[:, t : t + 1])
            nc.scalar.activation(shared[t][:], pw[t][:].indirect(l6[:]), COPY, scale=sb_sb[:, t : t + 1])
        hid = keep.tile([P, PACK, O], BF16, name="hid")
        hx = keep.tile([P, O, PACK], BF16, name="hx", align_bytes=64)
        for t in range(PACK):
            pg = keep.tile([P, S], F32, name="pg%d" % t)
            nc.vector.tensor_tensor(pg[:], own[t][:], shared[t][:], MAX)
            nc.scalar.activation(hid[:, t, :], pg[:].indirect(l7[:]), COPY, scale=sd_sb[:, t : t + 1])
        for t in range(0, PACK, 2):
            nc.vector.tensor_copy(hx[:, :, t : t + 2], hid[:, t : t + 2, :].rearrange("p t o -> p o t"))
        hq = keep.tile([P, O], U32, name="hq", align_bytes=64)
        hs = keep.tile([P, O], U8, name="hs", align_bytes=64)
        nc.vector.quantize_mx(out=hq[:].bitcast(FP8X4), scales=hs[:], in_=hx[:].rearrange("p o t -> p (o t)"))

        for u in range(N // P):
            acc = psum.tile([P, O], F32, name="y%d" % u)
            nc.tensor.matmul_mx(
                out=acc[:], lhsT=wbw[:, 2 * P * u : 2 * P * (u + 1)].bitcast(FP4X4), lhsT_scale=wbs[:, P * u : P * (u + 1)],
                rhs=hq[:].bitcast(FP8X4), rhs_scale=hs[:], start=True, stop=True,
            )
            res = keep.tile([P, O], F32, name="res%d" % u)
            if u == 0:
                nc.vector.tensor_copy(res[:], acc[:])
                nc.sync.dma_start(out[P * u : P * (u + 1), :], res[:])
            else:
                nc.scalar.copy(res[:], acc[:])
                nc.scalar.dma_start(out[P * u : P * (u + 1), :], res[:])
